import numpy as np
import ml_dtypes


def mxq(x, axis, fmt="e4m3"):
    dtype, down = {"e4m3": (ml_dtypes.float8_e4m3fn, 7), "e5m2": (ml_dtypes.float8_e5m2, 14)}[fmt]
    v = np.moveaxis(np.asarray(x, np.float32).astype(ml_dtypes.bfloat16).astype(np.float64), axis, -1)
    blocks = v.reshape(v.shape[:-1] + (-1, 32))
    amax = np.abs(blocks).max(-1, keepdims=True)
    byte = np.maximum(np.where(amax > 0, np.frexp(amax)[1] - 1 + 127, 0) - down, 1)
    scale = np.exp2(byte - 127.0)
    codes = (blocks / scale).astype(np.float32).astype(dtype).astype(np.float64)
    return np.moveaxis((codes * scale).reshape(v.shape), -1, axis)


WIDE = False


def mx_kscale(k):
    if not WIDE:
        return np.ones(k)
    levels = np.array([10, -10, 5, -5, 0])
    if k % 512:
        return np.exp2(np.random.permutation(np.resize(levels, k // 32))).repeat(32)
    a = np.empty((k // 512, 16))
    for p in range(k // 512):
        a[p, :8] = np.random.permutation(np.resize(levels, 8))
        for g in range(8):
            far = levels[np.abs(levels - a[p, g]) >= 10]
            a[p, g + 8] = far[np.random.randint(len(far))]
    return np.exp2(a.ravel()).repeat(32)


def f64(x):
    return np.asarray(x).astype(np.float64)


def striped(idx):
    return np.tile(idx.reshape(-1, 16).T, (8, 1)).astype(np.uint16)


def unstriped(offs):
    return offs[:16].T.reshape(-1).astype(np.int64)


E2M1 = np.array([0.0, 0.5, 1.0, 1.5, 2.0, 3.0, 4.0, 6.0, -0.0, -0.5, -1.0, -1.5, -2.0, -3.0, -4.0, -6.0])


def pack_weight(w, fmt):
    k, n = w.shape
    w = f64(np.asarray(w, np.float32).astype(ml_dtypes.bfloat16)).reshape(k // 32, 32, n)
    amax = np.abs(w).max(1)
    if fmt == "e4m3":
        byte = np.frexp(amax)[1] - 1 + 127 - 7
    else:
        mant, ex = np.frexp(amax / 6.0)
        byte = np.where(mant > 0.5, ex, ex - 1) + 127
    byte = np.clip(np.where(amax > 0, byte, 1), 1, 254)
    scaled = (w * np.exp2(127.0 - byte)[:, None, :]).reshape(k, n).astype(np.float32)
    by_word = np.ascontiguousarray(scaled.reshape(k // 512, 128, 4, n).transpose(0, 1, 3, 2))
    if fmt == "e4m3":
        words = by_word.astype(ml_dtypes.float8_e4m3fn).view(np.uint8)
    else:
        c = by_word.astype(ml_dtypes.float4_e2m1fn).view(np.uint8) & 0xF
        words = (c[..., 0::2] | (c[..., 1::2] << 4)).reshape(k // 512, 128, 2 * n)
    return np.ascontiguousarray(words), np.ascontiguousarray(byte.astype(np.uint8).reshape(k // 512, 16, n))


def unpack_weight(words, scales, fmt):
    g, _, n = scales.shape
    words = np.ascontiguousarray(words).reshape(g, 128, n, -1)
    if fmt == "e4m3":
        vals = words.view(ml_dtypes.float8_e4m3fn).astype(np.float64)
    else:
        nib = np.empty((g, 128, n, 4), np.uint8)
        nib[..., 0::2] = words & 0xF
        nib[..., 1::2] = words >> 4
        vals = E2M1[nib]
    vals = vals * np.repeat(np.exp2(scales.astype(np.float64) - 127.0), 8, axis=1)[..., None]
    return vals.transpose(0, 1, 3, 2).reshape(g * 512, n)


K, T, E, C, N = 1536, 1280, 6, 128, 128
K8 = 512


def by_expert(wq, xq):
    return np.concatenate([wq[e].T @ xq[:, e * C:(e + 1) * C] for e in range(E)], axis=1)


def setup_inputs():
    n = np.random.standard_normal
    s = mx_kscale(K)[:, None]
    w = n((E, K, N)) / np.sqrt(K) / s[None]
    w8 = [pack_weight(m[:K8], "e4m3") for m in w]
    w4 = [pack_weight(m[K8:], "e2m1") for m in w]
    return {
        "xT": (n((K, T)) * s).astype(np.float32),
        "xr": n((N, T)).astype(np.float32),
        "w8_words": np.stack([m[0] for m in w8]),
        "w8_scales": np.stack([m[1] for m in w8]),
        "w4_words": np.stack([m[0] for m in w4]),
        "w4_scales": np.stack([m[1] for m in w4]),
        "b": (0.3 * n((N, E))).astype(np.float32),
        "gate": np.tile(np.random.uniform(0.2, 1.0, E * C), (N, 1)).astype(np.float32),
        "offs": striped(np.random.permutation(T)[:E * C]),
    }


def reference(xT, xr, w8_words, w8_scales, w4_words, w4_scales, b, gate, offs):
    idx = unstriped(offs)
    w = np.stack([np.concatenate([unpack_weight(w8_words[e], w8_scales[e], "e4m3"), unpack_weight(w4_words[e], w4_scales[e], "e2m1")]) for e in range(E)])
    xq = mxq(f64(xT)[:, idx], 0, "e4m3")
    y = by_expert(w, xq)
    y = y + np.repeat(f64(b), C, axis=1)
    out = f64(xr).copy()
    out[:, idx] += f64(gate) * y
    return out

@@ -1,0 +1,153 @@
+from contextlib import ExitStack
+
+import concourse.mybir as mybir
+
+K, T, E, C, N = 1536, 1280, 6, 128, 128
+S = E * C
+P = 128
+FLOPS = 2 * S * K * N
+
+F32 = mybir.dt.float32
+BF16 = mybir.dt.bfloat16
+I32 = mybir.dt.int32
+U32 = mybir.dt.uint32
+U16 = mybir.dt.uint16
+U8 = mybir.dt.uint8
+FP8X4 = mybir.dt.float8_e4m3fn_x4
+FP4X4 = mybir.dt.float4_e2m1fn_x4
+COPY = mybir.ActivationFunctionType.Copy
+IDENT = mybir.ActivationFunctionType.Identity
+ADD = mybir.AluOpType.add
+MULT = mybir.AluOpType.mult
+
+CHUNKS = ((256, 512, 512), (512, 512, 256), (512, 512, 256))
+SHARE = ((200, 400, 400), (400, 400, 200), (400, 400, 88))
+PIECES = (2, 2, 2)
+HALVES = (640, 640)
+
+
+def tile_moe_res_lin_bias_kernel(tc, xT, xr, w8_words, w8_scales, w4_words, w4_scales, b, gate, offs, out):
+    nc = tc.nc
+    with ExitStack() as ctx:
+        keep = ctx.enter_context(tc.tile_pool(name="keep", bufs=1))
+        psum = ctx.enter_context(tc.psum_pool(name="psum", bufs=1))
+
+        offs_t = keep.tile([P, S // 16], U16, name="offs_t")
+        raw, grp = {}, {}
+        for a in range(3):
+            t0 = 0
+            for i, w in enumerate(CHUNKS[a]):
+                raw[a, i] = keep.tile([P, 4, w], F32, name=f"raw{a}_{i}", align_bytes=64)
+                grp[a, i] = keep.tile([P, w, 4], BF16, name=f"grp{a}_{i}", align_bytes=64)
+        codes = [keep.tile([P, T], U32, name=f"codes{a}", align_bytes=64) for a in range(3)]
+        words = [keep.tile([P, S], U32, name=f"words{a}", align_bytes=64) for a in range(3)]
+        sc01 = keep.tile([P, T], U8, name="sc01", align_bytes=64)
+        sc2 = keep.tile([P, T], U8, name="sc2", align_bytes=64)
+        by01 = keep.tile([P, S], U8, name="by01", align_bytes=64)
+        by2 = keep.tile([P, S], U8, name="by2", align_bytes=64)
+        planes = [sc01, sc2]
+        q_scale = [sc01[4:P, :], sc01[:], sc2[:]]
+        g_scale = [by01[4:P, :], by01[:], by2[:]]
+        byte_jobs = {1: (by01, sc01), 2: (by2, sc2)}
+        w8 = keep.tile([P, E, 4 * N], U8, name="w8", align_bytes=64)
+        w4 = keep.tile([P, E, 2, 2 * N], U8, name="w4", align_bytes=64)
+        w8s = keep.tile([P, E, N], U8, name="w8s", align_bytes=64)
+        w4s = keep.tile([P, E, 2, N], U8, name="w4s", align_bytes=64)
+        b_t = keep.tile([P, 8], F32, name="b_t")
+        gate_t = keep.tile([P, S], F32, name="gate_t", align_bytes=64)
+        xr_t = keep.tile([P, T], F32, name="xr_t", align_bytes=64)
+        win = keep.tile([P, T], F32, name="win", align_bytes=64)
+        o_t = keep.tile([P, T], F32, name="o_t", align_bytes=64)
+        acc = [psum.tile([P, C], F32, name=f"acc{e}") for e in range(E)]
+
+        nc.vector.memset(w8s[:].rearrange("p e n -> p (e n)").bitcast(I32), 0)
+        nc.vector.memset(w4s[:].rearrange("p e a n -> p (e a n)").bitcast(I32), 0)
+        for t in planes:
+            nc.gpsimd.memset(t[:], 0)
+        nc.gpsimd.memset(win[:], 0.0)
+
+        def load_x(a, i):
+            t0 = sum(CHUNKS[a][:i])
+            w = CHUNKS[a][i]
+            nc.sync.dma_start(raw[a, i][:], xT[512 * a : 512 * (a + 1), t0 : t0 + w].rearrange("(p j) t -> p j t", j=4))
+
+        load_x(0, 0)
+        nc.sync.dma_start(offs_t[:], offs)
+        order = [(a, i) for a in range(3) for i in range(len(CHUNKS[a]))]
+        for a, i in order[1:]:
+            load_x(a, i)
+        w8s_src = w8_scales.bitcast(I32)
+        w4s_src = w4_scales.bitcast(I32)
+        for q in range(4):
+            nc.sync.dma_start(w8s[32 * q : 32 * q + 4].rearrange("p e n -> p (e n)").bitcast(I32).rearrange("p (e n) -> p e n", e=E), w8s_src[:, :, 4 * q : 4 * q + 4, :].rearrange("e a q n -> q (e a) n"))
+        for q in range(4):
+            nc.sync.dma_start(w4s[32 * q : 32 * q + 4].rearrange("p e a n -> p (e a n)").bitcast(I32).rearrange("p (f n) -> p f n", f=2 * E), w4s_src[:, :, 4 * q : 4 * q + 4, :].rearrange("e a q n -> q (e a) n"))
+        nc.sync.dma_start(w8[:].rearrange("p e n -> p (e n)").bitcast(I32).rearrange("p (e n) -> p e n", e=E), w8_words.bitcast(I32).rearrange("e a p n r -> p (e a) (n r)"))
+        nc.sync.dma_start(w4[:].rearrange("p e a n -> p (e a n)").bitcast(I32).rearrange("p (f n) -> p f n", f=2 * E), w4_words.bitcast(I32).rearrange("e a p n -> p (e a) n"))
+        nc.sync.dma_start(b_t[:, 0:E], b)
+        nc.sync.dma_start(gate_t[:], gate)
+        nc.sync.dma_start(xr_t[:], xr)
+
+        def cast(a, i):
+            w = CHUNKS[a][i]
+            s = SHARE[a][i]
+            dst = grp[a, i][:].rearrange("p (c i) t -> p c t i", i=4)
+            src = raw[a, i][:].rearrange("p t (c i) -> p c t i", i=4)
+            if s > 0:
+                nc.scalar.activation(dst[:, 0 : s // 4], src[:, 0 : s // 4], COPY)
+            if s < w:
+                nc.vector.tensor_copy(dst[:, s // 4 : w // 4], src[:, s // 4 : w // 4])
+
+        def quantize(a, i):
+            t0 = sum(CHUNKS[a][:i])
+            w = CHUNKS[a][i]
+            nc.vector.quantize_mx(out=codes[a][:, t0 : t0 + w].bitcast(FP8X4), scales=q_scale[a][:, t0 : t0 + w], in_=grp[a, i][:].rearrange("p t j -> p (t j)"))
+
+        def gather(dst, src, s0, s1):
+            nc.vector.tensor_copy(dst[:, s0:s1], src[:].indirect(offs_t[:, s0 // 16 : s1 // 16]))
+
+        def multiply(a, e):
+            cols = slice(e * C, (e + 1) * C)
+            if a == 0:
+                lhs, lhs_scale = w8[:, e, :].bitcast(FP8X4), w8s[:, e, :]
+            else:
+                lhs, lhs_scale = w4[:, e, a - 1, :].bitcast(FP4X4), w4s[:, e, a - 1, :]
+            nc.tensor.matmul_mx(acc[e][:], lhs, lhs_scale, words[a][:, cols].bitcast(FP8X4), g_scale[a][:, cols], start=(a == 0), stop=(a == 2))
+
+        pending = []
+        for a, i in order:
+            cast(a, i)
+            for job in pending:
+                job()
+            pending = [lambda a=a, i=i: quantize(a, i)]
+            if i == len(CHUNKS[a]) - 1 and a < 2:
+                pending.append(lambda a=a: gather(words[a], codes[a], 0, S))
+                if a in byte_jobs:
+                    pending.append(lambda a=a: gather(byte_jobs[a][0], byte_jobs[a][1], 0, S))
+        for job in pending:
+            job()
+        for a in range(2):
+            for e in range(E):
+                multiply(a, e)
+        y = {}
+        s0 = 0
+        for k, n in enumerate(PIECES):
+            s1 = s0 + n * C
+            gather(words[2], codes[2], s0, s1)
+            gather(by2, sc2, s0, s1)
+            y[k] = keep.tile([P, n * C], F32, name=f"y{k}", align_bytes=64)
+            for e in range(s0 // C, s1 // C):
+                multiply(2, e)
+                off = e * C - s0
+                nc.scalar.activation(y[k][:, off : off + C], acc[e][:], IDENT, bias=b_t[:, e : e + 1])
+            s0 = s1
+        s0 = 0
+        for k, n in enumerate(PIECES):
+            s1 = s0 + n * C
+            nc.vector.tensor_tensor(win[:].indirect(offs_t[:, s0 // 16 : s1 // 16]), y[k][:], gate_t[:, s0:s1], MULT)
+            s0 = s1
+        t0 = 0
+        for h in HALVES:
+            nc.vector.tensor_tensor(o_t[:, t0 : t0 + h], win[:, t0 : t0 + h], xr_t[:, t0 : t0 + h], ADD)
+            nc.sync.dma_start(out[:, t0 : t0 + h], o_t[:, t0 : t0 + h])
+            t0 += h

@@ -20,9 +20,28 @@ IDENT = mybir.ActivationFunctionType.Identity
 ADD = mybir.AluOpType.add
 MULT = mybir.AluOpType.mult
 
-CHUNKS = ((256, 512, 512), (512, 512, 256), (512, 512, 256))
-SHARE = ((200, 400, 400), (400, 400, 200), (400, 400, 88))
-PIECES = (2, 2, 2)
+CHUNKS = ((256, 1024), (768, 512), (512, 512, 256))
+SHARE = ((192, 304), (560, 208), (448, 320, 256))
+PIECES = (2, 4)
+STEPS = (
+    ("c", 0, 0),
+    ("q", 0, 0),
+    ("c", 0, 1),
+    ("q", 0, 1),
+    ("c", 1, 0),
+    ("w", 0),
+    ("c", 1, 1),
+    ("q", 1, 0),
+    ("q", 1, 1),
+    ("w", 1),
+    ("c", 2, 0),
+    ("b"),
+    ("c", 2, 1),
+    ("q", 2, 0),
+    ("q", 2, 1),
+    ("c", 2, 2),
+    ("q", 2, 2),
+)
 HALVES = (640, 640)
 
 
@@ -49,8 +68,9 @@ def tile_moe_res_lin_bias_kernel(tc, xT, xr, w8_words, w8_scales, w4_words, w4_s
         q_scale = [sc01[4:P, :], sc01[:], sc2[:]]
         g_scale = [by01[4:P, :], by01[:], by2[:]]
         byte_jobs = {1: (by01, sc01), 2: (by2, sc2)}
-        w8 = keep.tile([P, E, 4 * N], U8, name="w8", align_bytes=64)
-        w4 = keep.tile([P, E, 2, 2 * N], U8, name="w4", align_bytes=64)
+        starts = [sum(PIECES[:k]) for k in range(len(PIECES))]
+        w8 = [keep.tile([P, n, 4 * N], U8, name=f"w8_{k}", align_bytes=64) for k, n in enumerate(PIECES)]
+        w4 = [keep.tile([P, n, 2, 2 * N], U8, name=f"w4_{k}", align_bytes=64) for k, n in enumerate(PIECES)]
         w8s = keep.tile([P, E, N], U8, name="w8s", align_bytes=64)
         w4s = keep.tile([P, E, 2, N], U8, name="w4s", align_bytes=64)
         b_t = keep.tile([P, 8], F32, name="b_t")
@@ -82,8 +102,13 @@ def tile_moe_res_lin_bias_kernel(tc, xT, xr, w8_words, w8_scales, w4_words, w4_s
             nc.sync.dma_start(w8s[32 * q : 32 * q + 4].rearrange("p e n -> p (e n)").bitcast(I32).rearrange("p (e n) -> p e n", e=E), w8s_src[:, :, 4 * q : 4 * q + 4, :].rearrange("e a q n -> q (e a) n"))
         for q in range(4):
             nc.sync.dma_start(w4s[32 * q : 32 * q + 4].rearrange("p e a n -> p (e a n)").bitcast(I32).rearrange("p (f n) -> p f n", f=2 * E), w4s_src[:, :, 4 * q : 4 * q + 4, :].rearrange("e a q n -> q (e a) n"))
-        nc.sync.dma_start(w8[:].rearrange("p e n -> p (e n)").bitcast(I32).rearrange("p (e n) -> p e n", e=E), w8_words.bitcast(I32).rearrange("e a p n r -> p (e a) (n r)"))
-        nc.sync.dma_start(w4[:].rearrange("p e a n -> p (e a n)").bitcast(I32).rearrange("p (f n) -> p f n", f=2 * E), w4_words.bitcast(I32).rearrange("e a p n -> p (e a) n"))
+        def load_w(k):
+            n, e0 = PIECES[k], starts[k]
+            nc.sync.dma_start(w8[k][:].rearrange("p e n -> p (e n)").bitcast(I32).rearrange("p (e n) -> p e n", e=n), w8_words.bitcast(I32)[e0 : e0 + n].rearrange("e a p n r -> p (e a) (n r)"))
+            nc.sync.dma_start(w4[k][:].rearrange("p e a n -> p (e a n)").bitcast(I32).rearrange("p (f n) -> p f n", f=2 * n), w4_words.bitcast(I32)[e0 : e0 + n].rearrange("e a p n -> p (e a) n"))
+
+        for k in range(len(PIECES)):
+            load_w(k)
         nc.sync.dma_start(b_t[:, 0:E], b)
         nc.sync.dma_start(gate_t[:], gate)
         nc.sync.dma_start(xr_t[:], xr)
@@ -101,34 +126,33 @@ def tile_moe_res_lin_bias_kernel(tc, xT, xr, w8_words, w8_scales, w4_words, w4_s
         def quantize(a, i):
             t0 = sum(CHUNKS[a][:i])
             w = CHUNKS[a][i]
-            nc.vector.quantize_mx(out=codes[a][:, t0 : t0 + w].bitcast(FP8X4), scales=q_scale[a][:, t0 : t0 + w], in_=grp[a, i][:].rearrange("p t j -> p (t j)"))
+            done = 0
+            while done < w:
+                n = min(512, w - done)
+                nc.vector.quantize_mx(out=codes[a][:, t0 + done : t0 + done + n].bitcast(FP8X4), scales=q_scale[a][:, t0 + done : t0 + done + n], in_=grp[a, i][:, done : done + n, :].rearrange("p t j -> p (t j)"))
+                done += n
 
         def gather(dst, src, s0, s1):
             nc.vector.tensor_copy(dst[:, s0:s1], src[:].indirect(offs_t[:, s0 // 16 : s1 // 16]))
 
         def multiply(a, e):
             cols = slice(e * C, (e + 1) * C)
+            k = max(k for k in range(len(PIECES)) if starts[k] <= e)
             if a == 0:
-                lhs, lhs_scale = w8[:, e, :].bitcast(FP8X4), w8s[:, e, :]
+                lhs, lhs_scale = w8[k][:, e - starts[k], :].bitcast(FP8X4), w8s[:, e, :]
             else:
-                lhs, lhs_scale = w4[:, e, a - 1, :].bitcast(FP4X4), w4s[:, e, a - 1, :]
+                lhs, lhs_scale = w4[k][:, e - starts[k], a - 1, :].bitcast(FP4X4), w4s[:, e, a - 1, :]
             nc.tensor.matmul_mx(acc[e][:], lhs, lhs_scale, words[a][:, cols].bitcast(FP8X4), g_scale[a][:, cols], start=(a == 0), stop=(a == 2))
 
-        pending = []
-        for a, i in order:
-            cast(a, i)
-            for job in pending:
-                job()
-            pending = [lambda a=a, i=i: quantize(a, i)]
-            if i == len(CHUNKS[a]) - 1 and a < 2:
-                pending.append(lambda a=a: gather(words[a], codes[a], 0, S))
-                if a in byte_jobs:
-                    pending.append(lambda a=a: gather(byte_jobs[a][0], byte_jobs[a][1], 0, S))
-        for job in pending:
-            job()
-        for a in range(2):
-            for e in range(E):
-                multiply(a, e)
+        for op in STEPS:
+            if op[0] == "c":
+                cast(op[1], op[2])
+            elif op[0] == "q":
+                quantize(op[1], op[2])
+            elif op[0] == "w":
+                gather(words[op[1]], codes[op[1]], 0, S)
+            else:
+                gather(by01, sc01, 0, S)
         y = {}
         s0 = 0
         for k, n in enumerate(PIECES):
@@ -136,6 +160,9 @@ def tile_moe_res_lin_bias_kernel(tc, xT, xr, w8_words, w8_scales, w4_words, w4_s
             gather(words[2], codes[2], s0, s1)
             gather(by2, sc2, s0, s1)
             y[k] = keep.tile([P, n * C], F32, name=f"y{k}", align_bytes=64)
+            for e in range(s0 // C, s1 // C):
+                multiply(0, e)
+                multiply(1, e)
             for e in range(s0 // C, s1 // C):
                 multiply(2, e)
                 off = e * C - s0

@@ -22,6 +22,8 @@ MULT = mybir.AluOpType.mult
 
 CHUNKS = ((256, 1024), (768, 512), (512, 512, 256))
 SHARE = ((192, 304), (560, 208), (448, 320, 256))
+LATE = 5
+GROUPS = (2, 3, 1)
 PIECES = (2, 4)
 STEPS = (
     ("c", 0, 0),
@@ -42,7 +44,7 @@ STEPS = (
     ("c", 2, 2),
     ("q", 2, 2),
 )
-HALVES = (640, 640)
+HALVES = (512, 448, 320)
 
 
 def tile_moe_res_lin_bias_kernel(tc, xT, xr, w8_words, w8_scales, w4_words, w4_scales, b, gate, offs, out):
@@ -68,9 +70,9 @@ def tile_moe_res_lin_bias_kernel(tc, xT, xr, w8_words, w8_scales, w4_words, w4_s
         q_scale = [sc01[4:P, :], sc01[:], sc2[:]]
         g_scale = [by01[4:P, :], by01[:], by2[:]]
         byte_jobs = {1: (by01, sc01), 2: (by2, sc2)}
-        starts = [sum(PIECES[:k]) for k in range(len(PIECES))]
-        w8 = [keep.tile([P, n, 4 * N], U8, name=f"w8_{k}", align_bytes=64) for k, n in enumerate(PIECES)]
-        w4 = [keep.tile([P, n, 2, 2 * N], U8, name=f"w4_{k}", align_bytes=64) for k, n in enumerate(PIECES)]
+        starts = [sum(GROUPS[:k]) for k in range(len(GROUPS))]
+        w8 = [keep.tile([P, n, 4 * N], U8, name=f"w8_{k}", align_bytes=64) for k, n in enumerate(GROUPS)]
+        w4 = [keep.tile([P, n, 2, 2 * N], U8, name=f"w4_{k}", align_bytes=64) for k, n in enumerate(GROUPS)]
         w8s = keep.tile([P, E, N], U8, name="w8s", align_bytes=64)
         w4s = keep.tile([P, E, 2, N], U8, name="w4s", align_bytes=64)
         b_t = keep.tile([P, 8], F32, name="b_t")
@@ -103,14 +105,15 @@ def tile_moe_res_lin_bias_kernel(tc, xT, xr, w8_words, w8_scales, w4_words, w4_s
         for q in range(4):
             nc.sync.dma_start(w4s[32 * q : 32 * q + 4].rearrange("p e a n -> p (e a n)").bitcast(I32).rearrange("p (f n) -> p f n", f=2 * E), w4s_src[:, :, 4 * q : 4 * q + 4, :].rearrange("e a q n -> q (e a) n"))
         def load_w(k):
-            n, e0 = PIECES[k], starts[k]
+            n, e0 = GROUPS[k], starts[k]
             nc.sync.dma_start(w8[k][:].rearrange("p e n -> p (e n)").bitcast(I32).rearrange("p (e n) -> p e n", e=n), w8_words.bitcast(I32)[e0 : e0 + n].rearrange("e a p n r -> p (e a) (n r)"))
             nc.sync.dma_start(w4[k][:].rearrange("p e a n -> p (e a n)").bitcast(I32).rearrange("p (f n) -> p f n", f=2 * n), w4_words.bitcast(I32)[e0 : e0 + n].rearrange("e a p n -> p (e a) n"))
 
-        for k in range(len(PIECES)):
+        for k in range(len(GROUPS)):
+            if k == 2:
+                nc.sync.dma_start(b_t[:, 0:E], b)
+                nc.sync.dma_start(gate_t[:], gate)
             load_w(k)
-        nc.sync.dma_start(b_t[:, 0:E], b)
-        nc.sync.dma_start(gate_t[:], gate)
         nc.sync.dma_start(xr_t[:], xr)
 
         def cast(a, i):
@@ -135,14 +138,14 @@ def tile_moe_res_lin_bias_kernel(tc, xT, xr, w8_words, w8_scales, w4_words, w4_s
         def gather(dst, src, s0, s1):
             nc.vector.tensor_copy(dst[:, s0:s1], src[:].indirect(offs_t[:, s0 // 16 : s1 // 16]))
 
-        def multiply(a, e):
+        def multiply(a, e, start, stop):
             cols = slice(e * C, (e + 1) * C)
-            k = max(k for k in range(len(PIECES)) if starts[k] <= e)
+            k = max(k for k in range(len(GROUPS)) if starts[k] <= e)
             if a == 0:
                 lhs, lhs_scale = w8[k][:, e - starts[k], :].bitcast(FP8X4), w8s[:, e, :]
             else:
                 lhs, lhs_scale = w4[k][:, e - starts[k], a - 1, :].bitcast(FP4X4), w4s[:, e, a - 1, :]
-            nc.tensor.matmul_mx(acc[e][:], lhs, lhs_scale, words[a][:, cols].bitcast(FP8X4), g_scale[a][:, cols], start=(a == 0), stop=(a == 2))
+            nc.tensor.matmul_mx(acc[e][:], lhs, lhs_scale, words[a][:, cols].bitcast(FP8X4), g_scale[a][:, cols], start=start, stop=stop)
 
         for op in STEPS:
             if op[0] == "c":
@@ -161,10 +164,16 @@ def tile_moe_res_lin_bias_kernel(tc, xT, xr, w8_words, w8_scales, w4_words, w4_s
             gather(by2, sc2, s0, s1)
             y[k] = keep.tile([P, n * C], F32, name=f"y{k}", align_bytes=64)
             for e in range(s0 // C, s1 // C):
-                multiply(0, e)
-                multiply(1, e)
+                if e < LATE:
+                    multiply(0, e, True, False)
+                    multiply(1, e, False, False)
             for e in range(s0 // C, s1 // C):
-                multiply(2, e)
+                if e < LATE:
+                    multiply(2, e, False, True)
+                else:
+                    multiply(2, e, True, False)
+                    multiply(0, e, False, False)
+                    multiply(1, e, False, True)
                 off = e * C - s0
                 nc.scalar.activation(y[k][:, off : off + C], acc[e][:], IDENT, bias=b_t[:, e : e + 1])
             s0 = s1

from contextlib import ExitStack

import concourse.mybir as mybir

K, T, E, C, N = 1536, 1280, 6, 128, 128
S = E * C
P = 128
FLOPS = 2 * S * K * N

F32 = mybir.dt.float32
BF16 = mybir.dt.bfloat16
I32 = mybir.dt.int32
U32 = mybir.dt.uint32
U16 = mybir.dt.uint16
U8 = mybir.dt.uint8
FP8X4 = mybir.dt.float8_e4m3fn_x4
FP4X4 = mybir.dt.float4_e2m1fn_x4
COPY = mybir.ActivationFunctionType.Copy
IDENT = mybir.ActivationFunctionType.Identity
ADD = mybir.AluOpType.add
MULT = mybir.AluOpType.mult

CHUNKS = ((256, 1024), (768, 512), (512, 512, 256))
SHARE = ((192, 304), (560, 208), (448, 320, 256))
LATE = 5
GROUPS = (2, 3, 1)
PIECES = (2, 4)
STEPS = (
    ("c", 0, 0),
    ("q", 0, 0),
    ("c", 0, 1),
    ("q", 0, 1),
    ("c", 1, 0),
    ("w", 0),
    ("c", 1, 1),
    ("q", 1, 0),
    ("q", 1, 1),
    ("w", 1),
    ("c", 2, 0),
    ("b"),
    ("c", 2, 1),
    ("q", 2, 0),
    ("q", 2, 1),
    ("c", 2, 2),
    ("q", 2, 2),
)
HALVES = (512, 448, 320)


def tile_moe_res_lin_bias_kernel(tc, xT, xr, w8_words, w8_scales, w4_words, w4_scales, b, gate, offs, out):
    nc = tc.nc
    with ExitStack() as ctx:
        keep = ctx.enter_context(tc.tile_pool(name="keep", bufs=1))
        psum = ctx.enter_context(tc.psum_pool(name="psum", bufs=1))

        offs_t = keep.tile([P, S // 16], U16, name="offs_t")
        raw, grp = {}, {}
        for a in range(3):
            t0 = 0
            for i, w in enumerate(CHUNKS[a]):
                raw[a, i] = keep.tile([P, 4, w], F32, name=f"raw{a}_{i}", align_bytes=64)
                grp[a, i] = keep.tile([P, w, 4], BF16, name=f"grp{a}_{i}", align_bytes=64)
        codes = [keep.tile([P, T], U32, name=f"codes{a}", align_bytes=64) for a in range(3)]
        words = [keep.tile([P, S], U32, name=f"words{a}", align_bytes=64) for a in range(3)]
        sc01 = keep.tile([P, T], U8, name="sc01", align_bytes=64)
        sc2 = keep.tile([P, T], U8, name="sc2", align_bytes=64)
        by01 = keep.tile([P, S], U8, name="by01", align_bytes=64)
        by2 = keep.tile([P, S], U8, name="by2", align_bytes=64)
        planes = [sc01, sc2]
        q_scale = [sc01[4:P, :], sc01[:], sc2[:]]
        g_scale = [by01[4:P, :], by01[:], by2[:]]
        byte_jobs = {1: (by01, sc01), 2: (by2, sc2)}
        starts = [sum(GROUPS[:k]) for k in range(len(GROUPS))]
        w8 = [keep.tile([P, n, 4 * N], U8, name=f"w8_{k}", align_bytes=64) for k, n in enumerate(GROUPS)]
        w4 = [keep.tile([P, n, 2, 2 * N], U8, name=f"w4_{k}", align_bytes=64) for k, n in enumerate(GROUPS)]
        w8s = keep.tile([P, E, N], U8, name="w8s", align_bytes=64)
        w4s = keep.tile([P, E, 2, N], U8, name="w4s", align_bytes=64)
        b_t = keep.tile([P, 8], F32, name="b_t")
        gate_t = keep.tile([P, S], F32, name="gate_t", align_bytes=64)
        xr_t = keep.tile([P, T], F32, name="xr_t", align_bytes=64)
        win = keep.tile([P, T], F32, name="win", align_bytes=64)
        o_t = keep.tile([P, T], F32, name="o_t", align_bytes=64)
        acc = [psum.tile([P, C], F32, name=f"acc{e}") for e in range(E)]

        nc.vector.memset(w8s[:].rearrange("p e n -> p (e n)").bitcast(I32), 0)
        nc.vector.memset(w4s[:].rearrange("p e a n -> p (e a n)").bitcast(I32), 0)
        for t in planes:
            nc.gpsimd.memset(t[:], 0)
        nc.gpsimd.memset(win[:], 0.0)

        def load_x(a, i):
            t0 = sum(CHUNKS[a][:i])
            w = CHUNKS[a][i]
            nc.sync.dma_start(raw[a, i][:], xT[512 * a : 512 * (a + 1), t0 : t0 + w].rearrange("(p j) t -> p j t", j=4))

        load_x(0, 0)
        nc.sync.dma_start(offs_t[:], offs)
        order = [(a, i) for a in range(3) for i in range(len(CHUNKS[a]))]
        for a, i in order[1:]:
            load_x(a, i)
        w8s_src = w8_scales.bitcast(I32)
        w4s_src = w4_scales.bitcast(I32)
        for q in range(4):
            nc.sync.dma_start(w8s[32 * q : 32 * q + 4].rearrange("p e n -> p (e n)").bitcast(I32).rearrange("p (e n) -> p e n", e=E), w8s_src[:, :, 4 * q : 4 * q + 4, :].rearrange("e a q n -> q (e a) n"))
        for q in range(4):
            nc.sync.dma_start(w4s[32 * q : 32 * q + 4].rearrange("p e a n -> p (e a n)").bitcast(I32).rearrange("p (f n) -> p f n", f=2 * E), w4s_src[:, :, 4 * q : 4 * q + 4, :].rearrange("e a q n -> q (e a) n"))
        def load_w(k):
            n, e0 = GROUPS[k], starts[k]
            nc.sync.dma_start(w8[k][:].rearrange("p e n -> p (e n)").bitcast(I32).rearrange("p (e n) -> p e n", e=n), w8_words.bitcast(I32)[e0 : e0 + n].rearrange("e a p n r -> p (e a) (n r)"))
            nc.sync.dma_start(w4[k][:].rearrange("p e a n -> p (e a n)").bitcast(I32).rearrange("p (f n) -> p f n", f=2 * n), w4_words.bitcast(I32)[e0 : e0 + n].rearrange("e a p n -> p (e a) n"))

        for k in range(len(GROUPS)):
            if k == 2:
                nc.sync.dma_start(b_t[:, 0:E], b)
                nc.sync.dma_start(gate_t[:], gate)
            load_w(k)
        nc.sync.dma_start(xr_t[:], xr)

        def cast(a, i):
            w = CHUNKS[a][i]
            s = SHARE[a][i]
            dst = grp[a, i][:].rearrange("p (c i) t -> p c t i", i=4)
            src = raw[a, i][:].rearrange("p t (c i) -> p c t i", i=4)
            if s > 0:
                nc.scalar.activation(dst[:, 0 : s // 4], src[:, 0 : s // 4], COPY)
            if s < w:
                nc.vector.tensor_copy(dst[:, s // 4 : w // 4], src[:, s // 4 : w // 4])

        def quantize(a, i):
            t0 = sum(CHUNKS[a][:i])
            w = CHUNKS[a][i]
            done = 0
            while done < w:
                n = min(512, w - done)
                nc.vector.quantize_mx(out=codes[a][:, t0 + done : t0 + done + n].bitcast(FP8X4), scales=q_scale[a][:, t0 + done : t0 + done + n], in_=grp[a, i][:, done : done + n, :].rearrange("p t j -> p (t j)"))
                done += n

        def gather(dst, src, s0, s1):
            nc.vector.tensor_copy(dst[:, s0:s1], src[:].indirect(offs_t[:, s0 // 16 : s1 // 16]))

        def multiply(a, e, start, stop):
            cols = slice(e * C, (e + 1) * C)
            k = max(k for k in range(len(GROUPS)) if starts[k] <= e)
            if a == 0:
                lhs, lhs_scale = w8[k][:, e - starts[k], :].bitcast(FP8X4), w8s[:, e, :]
            else:
                lhs, lhs_scale = w4[k][:, e - starts[k], a - 1, :].bitcast(FP4X4), w4s[:, e, a - 1, :]
            nc.tensor.matmul_mx(acc[e][:], lhs, lhs_scale, words[a][:, cols].bitcast(FP8X4), g_scale[a][:, cols], start=start, stop=stop)

        for op in STEPS:
            if op[0] == "c":
                cast(op[1], op[2])
            elif op[0] == "q":
                quantize(op[1], op[2])
            elif op[0] == "w":
                gather(words[op[1]], codes[op[1]], 0, S)
            else:
                gather(by01, sc01, 0, S)
        y = {}
        s0 = 0
        for k, n in enumerate(PIECES):
            s1 = s0 + n * C
            gather(words[2], codes[2], s0, s1)
            gather(by2, sc2, s0, s1)
            y[k] = keep.tile([P, n * C], F32, name=f"y{k}", align_bytes=64)
            for e in range(s0 // C, s1 // C):
                if e < LATE:
                    multiply(0, e, True, False)
                    multiply(1, e, False, False)
            for e in range(s0 // C, s1 // C):
                if e < LATE:
                    multiply(2, e, False, True)
                else:
                    multiply(2, e, True, False)
                    multiply(0, e, False, False)
                    multiply(1, e, False, True)
                off = e * C - s0
                nc.scalar.activation(y[k][:, off : off + C], acc[e][:], IDENT, bias=b_t[:, e : e + 1])
            s0 = s1
        s0 = 0
        for k, n in enumerate(PIECES):
            s1 = s0 + n * C
            nc.vector.tensor_tensor(win[:].indirect(offs_t[:, s0 // 16 : s1 // 16]), y[k][:], gate_t[:, s0:s1], MULT)
            s0 = s1
        t0 = 0
        for h in HALVES:
            nc.vector.tensor_tensor(o_t[:, t0 : t0 + h], win[:, t0 : t0 + h], xr_t[:, t0 : t0 + h], ADD)
            nc.sync.dma_start(out[:, t0 : t0 + h], o_t[:, t0 : t0 + h])
            t0 += h
